import numpy as np
import ml_dtypes


def mxq(x, axis, fmt="e4m3"):
    dtype, down = {"e4m3": (ml_dtypes.float8_e4m3fn, 7), "e5m2": (ml_dtypes.float8_e5m2, 14)}[fmt]
    v = np.moveaxis(np.asarray(x, np.float32).astype(ml_dtypes.bfloat16).astype(np.float64), axis, -1)
    blocks = v.reshape(v.shape[:-1] + (-1, 32))
    amax = np.abs(blocks).max(-1, keepdims=True)
    byte = np.maximum(np.where(amax > 0, np.frexp(amax)[1] - 1 + 127, 0) - down, 1)
    scale = np.exp2(byte - 127.0)
    codes = (blocks / scale).astype(np.float32).astype(dtype).astype(np.float64)
    return np.moveaxis((codes * scale).reshape(v.shape), -1, axis)


WIDE = False


def mx_kscale(k):
    if not WIDE:
        return np.ones(k)
    levels = np.array([10, -10, 5, -5, 0])
    if k % 512:
        return np.exp2(np.random.permutation(np.resize(levels, k // 32))).repeat(32)
    a = np.empty((k // 512, 16))
    for p in range(k // 512):
        a[p, :8] = np.random.permutation(np.resize(levels, 8))
        for g in range(8):
            far = levels[np.abs(levels - a[p, g]) >= 10]
            a[p, g + 8] = far[np.random.randint(len(far))]
    return np.exp2(a.ravel()).repeat(32)


def f64(x):
    return np.asarray(x).astype(np.float64)


def striped(idx):
    return np.tile(np.asarray(idx).reshape(-1, 16).T, (8, 1)).astype(np.uint16)


def unstriped(offs):
    return offs[:16].T.reshape(-1).astype(np.int64)


E2M1 = np.array([0.0, 0.5, 1.0, 1.5, 2.0, 3.0, 4.0, 6.0, -0.0, -0.5, -1.0, -1.5, -2.0, -3.0, -4.0, -6.0])


def pack_weight(w, fmt):
    k, n = w.shape
    w = f64(np.asarray(w, np.float32).astype(ml_dtypes.bfloat16)).reshape(k // 32, 32, n)
    amax = np.abs(w).max(1)
    if fmt == "e4m3":
        byte = np.frexp(amax)[1] - 1 + 127 - 7
    else:
        mant, ex = np.frexp(amax / 6.0)
        byte = np.where(mant > 0.5, ex, ex - 1) + 127
    byte = np.clip(np.where(amax > 0, byte, 1), 1, 254)
    scaled = (w * np.exp2(127.0 - byte)[:, None, :]).reshape(k, n).astype(np.float32)
    by_word = np.ascontiguousarray(scaled.reshape(k // 512, 128, 4, n).transpose(0, 1, 3, 2))
    if fmt == "e4m3":
        words = by_word.astype(ml_dtypes.float8_e4m3fn).view(np.uint8)
    else:
        c = by_word.astype(ml_dtypes.float4_e2m1fn).view(np.uint8) & 0xF
        words = (c[..., 0::2] | (c[..., 1::2] << 4)).reshape(k // 512, 128, 2 * n)
    return np.ascontiguousarray(words), np.ascontiguousarray(byte.astype(np.uint8).reshape(k // 512, 16, n))


def unpack_weight(words, scales, fmt):
    g, _, n = scales.shape
    words = np.ascontiguousarray(words).reshape(g, 128, n, -1)
    if fmt == "e4m3":
        vals = words.view(ml_dtypes.float8_e4m3fn).astype(np.float64)
    else:
        nib = np.empty((g, 128, n, 4), np.uint8)
        nib[..., 0::2] = words & 0xF
        nib[..., 1::2] = words >> 4
        vals = E2M1[nib]
    vals = vals * np.repeat(np.exp2(scales.astype(np.float64) - 127.0), 8, axis=1)[..., None]
    return vals.transpose(0, 1, 3, 2).reshape(g * 512, n)


def sigmoid(v):
    return 1.0 / (1.0 + np.exp(-v))


D, E, T, I, Q, G = 512, 512, 2048, 512, 128, 64


def setup_inputs():
    n = np.random.standard_normal
    idx = np.random.permutation(T)[:I]
    fd = mx_kscale(D)
    fe = mx_kscale(E)
    keysp = pack_weight(n((D, T)) / fd[:, None], "e2m1")
    valsp = pack_weight(n((E, T)) / fe[:, None], "e2m1")
    return {
        "query": (n((D, Q)) * 0.8 / np.sqrt(D) * fd[:, None]).astype(np.float32),
        "keys_words": keysp[0],
        "keys_scales": keysp[1],
        "th": (np.random.uniform(1.8, 2.8, (Q, 1))).astype(np.float32),
        "gout": (n((E, Q)) * 1 / np.sqrt(E) * fe[:, None]).astype(np.float32),
        "vals_words": valsp[0],
        "vals_scales": valsp[1],
        "dquery": (n((D, Q)) * 1.0 / np.sqrt(D) * fd[:, None]).astype(np.float32),
        "base": (0.5 * n((Q, T))).astype(np.float32),
        "offs": striped(idx),
    }


def reference(query, keys_words, keys_scales, th, gout, vals_words, vals_scales, dquery, base, offs):
    idx = unstriped(offs)
    keysu = unpack_weight(keys_words, keys_scales, "e2m1")
    valsu = unpack_weight(vals_words, vals_scales, "e2m1")
    queryq = mxq(f64(query), 0, "e4m3")
    keysidxg = keysu[:, idx]
    a = queryq.T @ keysidxg
    dqueryq = mxq(f64(dquery), 0, "e4m3")
    ta = dqueryq.T @ keysidxg
    p = np.exp(a)
    s = p.reshape(Q, G, I // G).sum(axis=2)
    sh = sigmoid(np.log(s) - f64(th)) / s
    sr = np.repeat(sh, I // G, axis=1)
    goutq = mxq(f64(gout), 0, "e4m3")
    valsidxg = valsu[:, idx]
    c0 = goutq.T @ valsidxg
    dsr = c0 * p
    dsh = dsr.reshape(Q, G, I // G).sum(axis=2)
    ds = dsh / s * sigmoid(np.log(s) - f64(th)) * (1.0 - sigmoid(np.log(s) - f64(th))) / s - dsh * sigmoid(np.log(s) - f64(th)) / np.square(s)
    r1 = np.repeat(ds, I // G, axis=1)
    dp = c0 * sr + r1
    tp = ta * p
    ts = tp.reshape(Q, G, I // G).sum(axis=2)
    tsh = (ts / s * sigmoid(np.log(s) - f64(th)) * (1.0 - sigmoid(np.log(s) - f64(th))) - ts * sigmoid(np.log(s) - f64(th)) / s) / s
    tsr = np.repeat(tsh, I // G, axis=1)
    tdsr = tp * c0
    tdsh = tdsr.reshape(Q, G, I // G).sum(axis=2)
    tds = (((tdsh - ts * dsh / s) / s * sigmoid(np.log(s) - f64(th)) + ts / s * sigmoid(np.log(s) - f64(th)) * (1.0 - sigmoid(np.log(s) - f64(th))) * dsh / s) * (1.0 - sigmoid(np.log(s) - f64(th))) + ts / s * sigmoid(np.log(s) - f64(th)) * (1.0 - sigmoid(np.log(s) - f64(th))) * (-1.0) * dsh / s * sigmoid(np.log(s) - f64(th)) - ts * dsh / s * sigmoid(np.log(s) - f64(th)) * (1.0 - sigmoid(np.log(s) - f64(th))) / s) / s - (tdsh * sigmoid(np.log(s) - f64(th)) + ts / s * sigmoid(np.log(s) - f64(th)) * (1.0 - sigmoid(np.log(s) - f64(th))) * dsh - ts * s * 2.0 * dsh * sigmoid(np.log(s) - f64(th)) / np.square(s)) / np.square(s)
    tr1 = np.repeat(tds, I // G, axis=1)
    tdp = tsr * c0 + tr1
    tda = tdp * p + tp * dp
    gs = tda * 8.0
    gf = np.zeros((Q, T))
    gf[:, idx] = gs
    y = f64(base) + gf
    return y

@@ -1,0 +1,149 @@
+from contextlib import ExitStack
+
+import concourse.mybir as mybir
+
+D, E, T, I, Q, G = 512, 512, 2048, 512, 128, 64
+GS = I // G
+FLOPS = 3 * 2 * 512 * Q * I
+
+F32 = mybir.dt.float32
+BF16 = mybir.dt.bfloat16
+I32 = mybir.dt.int32
+U32 = mybir.dt.uint32
+U16 = mybir.dt.uint16
+U8 = mybir.dt.uint8
+FP8X4 = mybir.dt.float8_e4m3fn_x4
+FP4X4 = mybir.dt.float4_e2m1fn_x4
+ALU = mybir.AluOpType
+ACT = mybir.ActivationFunctionType
+AX = mybir.AxisListType
+
+P = 128
+PACK = 4
+OUT_CHUNKS = (256, 512, 512, 512, 256)
+
+
+def tile_attend_hvgatedgroups_s_kernel(tc, query, keys_words, keys_scales, th, gout, vals_words, vals_scales, dquery, base, offs, out):
+    nc = tc.nc
+    with ExitStack() as ctx:
+        sb = ctx.enter_context(tc.tile_pool(name="sb", bufs=1))
+        ps = ctx.enter_context(tc.psum_pool(name="ps", bufs=1))
+
+        def grouped(ap):
+            return ap.rearrange("p (g j) -> p g j", j=GS)
+
+        def spread(ap):
+            return ap.unsqueeze(2).to_broadcast([P, G, GS])
+
+        offsets = sb.tile([P, I // 16], U16, name="offsets")
+        kw = sb.tile([P, T], U16, name="kw")
+        vw = sb.tile([P, T], U16, name="vw", tag="vw")
+        ks = sb.tile([P, T], U8, name="ks")
+        vs = sb.tile([P, T], U8, name="vs", tag="vs")
+        th_sb = sb.tile([P, 1], F32, name="th_sb")
+        base_sb = sb.tile([P, T], F32, name="base_sb")
+        window = sb.tile([P, T], F32, name="window")
+        raw = {n: sb.tile([P, PACK, Q], F32, name="raw_" + n) for n in ("q", "dq", "go")}
+        woven = {n: sb.tile([P, Q, PACK], BF16, name="woven_" + n, align_bytes=64) for n in ("q", "dq", "go")}
+        codes = {n: sb.tile([P, Q], U32, name="codes_" + n, align_bytes=64) for n in ("q", "dq", "go")}
+        scales = {n: sb.tile([P, Q], U8, name="scales_" + n, align_bytes=64) for n in ("q", "dq", "go")}
+        kwg = sb.tile([P, I], U16, name="kwg", align_bytes=64)
+        vwg = sb.tile([P, I], U16, name="vwg", align_bytes=64)
+        ksg = sb.tile([P, I], U8, name="ksg", align_bytes=64)
+        vsg = sb.tile([P, I], U8, name="vsg", align_bytes=64)
+
+        nc.gpsimd.memset(ks[:].bitcast(I32), 0)
+        nc.gpsimd.memset(vs[:].bitcast(I32), 0)
+        nc.vector.memset(window[:], 0.0)
+
+        def load_scales(tile, src):
+            for quad in range(4):
+                nc.sync.dma_start(out=tile[32 * quad : 32 * quad + 4, :].bitcast(I32), in_=src[0, 4 * quad : 4 * quad + 4, :].bitcast(I32))
+
+        def load_rows(n, src):
+            nc.sync.dma_start(out=raw[n][:], in_=src.rearrange("(p j) w -> p j w", j=PACK))
+
+        nc.sync.dma_start(offsets[:], offs)
+        nc.scalar.dma_start(out=th_sb[:], in_=th)
+        nc.sync.dma_start(out=kw[:].bitcast(I32), in_=keys_words[0].bitcast(I32))
+        load_scales(ks, keys_scales)
+        load_rows("q", query)
+        load_rows("dq", dquery)
+        nc.sync.dma_start(out=vw[:].bitcast(I32), in_=vals_words[0].bitcast(I32))
+        load_scales(vs, vals_scales)
+        load_rows("go", gout)
+        nc.sync.dma_start(out=base_sb[:], in_=base)
+
+        eth = sb.tile([P, 1], F32, name="eth")
+        nc.scalar.activation(eth[:], th_sb[:], ACT.Exp)
+
+        def weave(n):
+            nc.scalar.copy(out=woven[n][:], in_=raw[n][:].rearrange("p j w -> p w j"))
+
+        def quantize(n):
+            nc.vector.quantize_mx(out=codes[n][:].bitcast(FP8X4), scales=scales[n][:], in_=woven[n][:].rearrange("p w j -> p (w j)"))
+
+        def product(n, words, bytes_, name):
+            acc = ps.tile([Q, I], F32, name=name)
+            nc.tensor.matmul_mx(out=acc[:], lhsT=codes[n][:].bitcast(FP8X4), lhsT_scale=scales[n][:], rhs=words[:].bitcast(FP4X4), rhs_scale=bytes_[:], start=True, stop=True)
+            return acc
+
+        weave("q")
+        weave("dq")
+        nc.vector.tensor_copy(kwg[:], kw[:].indirect(offsets[:]))
+        nc.vector.tensor_copy(ksg[:], ks[:].indirect(offsets[:]))
+        quantize("q")
+        quantize("dq")
+        a = product("q", kwg, ksg, "a")
+        ta = product("dq", kwg, ksg, "ta")
+        p = sb.tile([P, I], F32, name="p")
+        nc.scalar.activation(p[:], a[:], ACT.Exp)
+        weave("go")
+
+        nc.vector.tensor_copy(vwg[:], vw[:].indirect(offsets[:]))
+        s = sb.tile([P, G], F32, name="s", tag="vw")
+        nc.vector.tensor_reduce(s[:], grouped(p[:]), AX.X, ALU.add)
+        nc.vector.tensor_copy(vsg[:], vs[:].indirect(offsets[:]))
+        root = sb.tile([P, G], F32, name="root")
+        nc.scalar.activation(root[:], s[:], ACT.Abs_reciprocal_sqrt, bias=eth[:])
+        quantize("go")
+        c = product("go", vwg, vsg, "c")
+        r = sb.tile([P, G], F32, name="r")
+        nc.scalar.activation(r[:], root[:], ACT.Square)
+
+        w = sb.tile([P, I], F32, name="w", tag="vs")
+        nc.vector.tensor_tensor(grouped(w[:]), grouped(p[:]), spread(r[:]), ALU.mult)
+        tw = sb.tile([P, I], F32, name="tw")
+        nc.vector.tensor_tensor(tw[:], ta[:], w[:], ALU.mult)
+        cw = sb.tile([P, I], F32, name="cw")
+        nc.vector.tensor_tensor(cw[:], c[:], w[:], ALU.mult)
+        u = sb.tile([P, G], F32, name="u")
+        nc.vector.tensor_reduce(u[:], grouped(tw[:]), AX.X, ALU.add)
+        tcw = sb.tile([P, I], F32, name="tcw")
+        nc.vector.tensor_tensor(tcw[:], c[:], tw[:], ALU.mult)
+        m = sb.tile([P, G], F32, name="m")
+        nc.vector.tensor_reduce(m[:], grouped(cw[:]), AX.X, ALU.add)
+        x = sb.tile([P, I], F32, name="x")
+        nc.vector.tensor_tensor(grouped(x[:]), grouped(ta[:]), spread(u[:]), ALU.subtract)
+        v = sb.tile([P, G], F32, name="v")
+        nc.vector.tensor_reduce(v[:], grouped(tcw[:]), AX.X, ALU.add)
+        um8 = sb.tile([P, G], F32, name="um8")
+        nc.vector.scalar_tensor_tensor(um8[:], u[:], 8.0, m[:], ALU.mult, ALU.mult)
+        y = sb.tile([P, I], F32, name="y")
+        nc.vector.tensor_tensor(grouped(y[:]), grouped(c[:]), spread(m[:]), ALU.subtract)
+        k8 = sb.tile([P, G], F32, name="k8")
+        nc.vector.scalar_tensor_tensor(k8[:], v[:], 8.0, um8[:], ALU.mult, ALU.subtract)
+        z = sb.tile([P, I], F32, name="z")
+        nc.vector.scalar_tensor_tensor(z[:], x[:], 8.0, y[:], ALU.mult, ALU.mult)
+        z2 = sb.tile([P, I], F32, name="z2")
+        nc.vector.tensor_tensor(grouped(z2[:]), grouped(z[:]), spread(k8[:]), ALU.subtract)
+        nc.vector.tensor_tensor(window[:].indirect(offsets[:]), z2[:], w[:], ALU.mult)
+
+        res = sb.tile([P, T], F32, name="res")
+        col = 0
+        for n, width in enumerate(OUT_CHUNKS):
+            cols = slice(col, col + width)
+            nc.vector.tensor_tensor(res[:, cols], window[:, cols], base_sb[:, cols], ALU.add)
+            queue = nc.sync if n % 2 == 0 else nc.scalar
+            queue.dma_start(out=out[:, cols], in_=res[:, cols])
+            col = col + width

@@ -37,15 +37,15 @@ def tile_attend_hvgatedgroups_s_kernel(tc, query, keys_words, keys_scales, th, g
 
         offsets = sb.tile([P, I // 16], U16, name="offsets")
         kw = sb.tile([P, T], U16, name="kw")
-        vw = sb.tile([P, T], U16, name="vw", tag="vw")
+        vw = sb.tile([P, T], U16, name="vw")
         ks = sb.tile([P, T], U8, name="ks")
-        vs = sb.tile([P, T], U8, name="vs", tag="vs")
+        vs = sb.tile([P, T], U8, name="vs", tag="codes_go", align_bytes=64)
         th_sb = sb.tile([P, 1], F32, name="th_sb")
         base_sb = sb.tile([P, T], F32, name="base_sb")
         window = sb.tile([P, T], F32, name="window")
-        raw = {n: sb.tile([P, PACK, Q], F32, name="raw_" + n) for n in ("q", "dq", "go")}
-        woven = {n: sb.tile([P, Q, PACK], BF16, name="woven_" + n, align_bytes=64) for n in ("q", "dq", "go")}
-        codes = {n: sb.tile([P, Q], U32, name="codes_" + n, align_bytes=64) for n in ("q", "dq", "go")}
+        raw = {n: sb.tile([P, PACK, Q], F32, name="raw_" + n, tag="raw_" + n) for n in ("q", "dq", "go")}
+        woven = {n: sb.tile([P, Q, PACK], BF16, name="woven_" + n, tag="woven_" + n, align_bytes=64) for n in ("q", "dq", "go")}
+        codes = {}
         scales = {n: sb.tile([P, Q], U8, name="scales_" + n, align_bytes=64) for n in ("q", "dq", "go")}
         kwg = sb.tile([P, I], U16, name="kwg", align_bytes=64)
         vwg = sb.tile([P, I], U16, name="vwg", align_bytes=64)
@@ -81,6 +81,7 @@ def tile_attend_hvgatedgroups_s_kernel(tc, query, keys_words, keys_scales, th, g
             nc.scalar.copy(out=woven[n][:], in_=raw[n][:].rearrange("p j w -> p w j"))
 
         def quantize(n):
+            codes[n] = sb.tile([P, Q], U32, name="codes_" + n, tag="codes_" + n, align_bytes=64)
             nc.vector.quantize_mx(out=codes[n][:].bitcast(FP8X4), scales=scales[n][:], in_=woven[n][:].rearrange("p w j -> p (w j)"))
 
         def product(n, words, bytes_, name):
@@ -100,43 +101,53 @@ def tile_attend_hvgatedgroups_s_kernel(tc, query, keys_words, keys_scales, th, g
         nc.scalar.activation(p[:], a[:], ACT.Exp)
         weave("go")
 
-        nc.vector.tensor_copy(vwg[:], vw[:].indirect(offsets[:]))
-        s = sb.tile([P, G], F32, name="s", tag="vw")
-        nc.vector.tensor_reduce(s[:], grouped(p[:]), AX.X, ALU.add)
-        nc.vector.tensor_copy(vsg[:], vs[:].indirect(offsets[:]))
-        root = sb.tile([P, G], F32, name="root")
+        half4 = sb.tile([P, G, 4], F32, name="half4")
+        half2 = sb.tile([P, G, 2], F32, name="half2")
+        s = sb.tile([P, G], F32, name="s")
+        nc.gpsimd.tensor_tensor(half4[:], grouped(p[:])[:, :, 0:4], grouped(p[:])[:, :, 4:8], ALU.add)
+        nc.gpsimd.tensor_tensor(half2[:], half4[:, :, 0:2], half4[:, :, 2:4], ALU.add)
+        nc.gpsimd.tensor_tensor(s[:], half2[:, :, 0], half2[:, :, 1], ALU.add)
+        root = sb.tile([P, G], F32, name="root", tag="raw_go")
         nc.scalar.activation(root[:], s[:], ACT.Abs_reciprocal_sqrt, bias=eth[:])
-        quantize("go")
-        c = product("go", vwg, vsg, "c")
         r = sb.tile([P, G], F32, name="r")
         nc.scalar.activation(r[:], root[:], ACT.Square)
+        w = sb.tile([P, I], F32, name="w")
+        nc.gpsimd.tensor_tensor(grouped(w[:]), grouped(p[:]), spread(r[:]), ALU.mult)
 
-        w = sb.tile([P, I], F32, name="w", tag="vs")
-        nc.vector.tensor_tensor(grouped(w[:]), grouped(p[:]), spread(r[:]), ALU.mult)
-        tw = sb.tile([P, I], F32, name="tw")
-        nc.vector.tensor_tensor(tw[:], ta[:], w[:], ALU.mult)
-        cw = sb.tile([P, I], F32, name="cw")
-        nc.vector.tensor_tensor(cw[:], c[:], w[:], ALU.mult)
-        u = sb.tile([P, G], F32, name="u")
-        nc.vector.tensor_reduce(u[:], grouped(tw[:]), AX.X, ALU.add)
-        tcw = sb.tile([P, I], F32, name="tcw")
-        nc.vector.tensor_tensor(tcw[:], c[:], tw[:], ALU.mult)
-        m = sb.tile([P, G], F32, name="m")
-        nc.vector.tensor_reduce(m[:], grouped(cw[:]), AX.X, ALU.add)
+        nc.vector.tensor_copy(vwg[:], vw[:].indirect(offsets[:]))
+        nc.vector.tensor_copy(vsg[:], vs[:].indirect(offsets[:]))
+        quantize("go")
+        c = product("go", vwg, vsg, "c")
+
+        sums = sb.tile([P, 3, G], F32, name="sums")
+        tp = sb.tile([P, I], F32, name="tp", tag="woven_go", align_bytes=64)
+        nc.vector.tensor_tensor(tp[:], ta[:], p[:], ALU.mult)
+        pc = sb.tile([P, I], F32, name="pc")
+        nc.vector.tensor_tensor(pc[:], c[:], p[:], ALU.mult)
+        nc.vector.tensor_reduce(sums[:, 0, :], grouped(tp[:]), AX.X, ALU.add)
+        tpc = sb.tile([P, I], F32, name="tpc")
+        nc.vector.tensor_tensor(tpc[:], c[:], tp[:], ALU.mult)
+        nc.vector.tensor_reduce(sums[:, 1, :], grouped(pc[:]), AX.X, ALU.add)
+        nc.vector.tensor_reduce(sums[:, 2, :], grouped(tpc[:]), AX.X, ALU.add)
+        means = sb.tile([P, 3, G], F32, name="means")
+        nc.vector.tensor_tensor(means[:], sums[:], r[:].unsqueeze(1).to_broadcast([P, 3, G]), ALU.mult)
+        u, m, v = means[:, 0, :], means[:, 1, :], means[:, 2, :]
         x = sb.tile([P, I], F32, name="x")
-        nc.vector.tensor_tensor(grouped(x[:]), grouped(ta[:]), spread(u[:]), ALU.subtract)
-        v = sb.tile([P, G], F32, name="v")
-        nc.vector.tensor_reduce(v[:], grouped(tcw[:]), AX.X, ALU.add)
+        nc.vector.tensor_tensor(grouped(x[:]), grouped(ta[:]), spread(u), ALU.subtract)
         um8 = sb.tile([P, G], F32, name="um8")
-        nc.vector.scalar_tensor_tensor(um8[:], u[:], 8.0, m[:], ALU.mult, ALU.mult)
+        nc.vector.scalar_tensor_tensor(um8[:], u, 8.0, m, ALU.mult, ALU.mult)
         y = sb.tile([P, I], F32, name="y")
-        nc.vector.tensor_tensor(grouped(y[:]), grouped(c[:]), spread(m[:]), ALU.subtract)
+        nc.vector.tensor_tensor(grouped(y[:]), grouped(c[:]), spread(m), ALU.subtract)
         k8 = sb.tile([P, G], F32, name="k8")
-        nc.vector.scalar_tensor_tensor(k8[:], v[:], 8.0, um8[:], ALU.mult, ALU.subtract)
+        nc.vector.scalar_tensor_tensor(k8[:], v, 8.0, um8[:], ALU.mult, ALU.subtract)
         z = sb.tile([P, I], F32, name="z")
-        nc.vector.scalar_tensor_tensor(z[:], x[:], 8.0, y[:], ALU.mult, ALU.mult)
         z2 = sb.tile([P, I], F32, name="z2")
-        nc.vector.tensor_tensor(grouped(z2[:]), grouped(z[:]), spread(k8[:]), ALU.subtract)
+        halves = (slice(0, I // 2), slice(I // 2, I))
+        for h in halves:
+            nc.vector.scalar_tensor_tensor(z[:, h], x[:, h], 8.0, y[:, h], ALU.mult, ALU.mult)
+        for n, h in enumerate(halves):
+            k_half = k8[:, n * G // 2 : (n + 1) * G // 2].unsqueeze(2).to_broadcast([P, G // 2, GS])
+            nc.vector.tensor_tensor(grouped(z2[:, h]), grouped(z[:, h]), k_half, ALU.subtract)
         nc.vector.tensor_tensor(window[:].indirect(offsets[:]), z2[:], w[:], ALU.mult)
 
         res = sb.tile([P, T], F32, name="res")

@@ -52,13 +52,13 @@ def tile_attend_hvgatedgroups_s_kernel(tc, query, keys_words, keys_scales, th, g
         ksg = sb.tile([P, I], U8, name="ksg", align_bytes=64)
         vsg = sb.tile([P, I], U8, name="vsg", align_bytes=64)
 
-        nc.gpsimd.memset(ks[:].bitcast(I32), 0)
-        nc.gpsimd.memset(vs[:].bitcast(I32), 0)
+        nc.vector.memset(ks[:].bitcast(I32), 0)
+        nc.vector.memset(vs[:].bitcast(I32), 0)
         nc.vector.memset(window[:], 0.0)
 
         def load_scales(tile, src):
-            for quad in range(4):
-                nc.sync.dma_start(out=tile[32 * quad : 32 * quad + 4, :].bitcast(I32), in_=src[0, 4 * quad : 4 * quad + 4, :].bitcast(I32))
+            for row in range(4):
+                nc.sync.dma_start(out=tile[row:P:32, :].bitcast(I32), in_=src[0, row:16:4, :].bitcast(I32))
 
         def load_rows(n, src):
             nc.sync.dma_start(out=raw[n][:], in_=src.rearrange("(p j) w -> p j w", j=PACK))

@@ -27,6 +27,7 @@ def tile_attend_hvgatedgroups_s_kernel(tc, query, keys_words, keys_scales, th, g
     nc = tc.nc
     with ExitStack() as ctx:
         sb = ctx.enter_context(tc.tile_pool(name="sb", bufs=1))
+        shared = ctx.enter_context(tc.tile_pool(name="shared", bufs=1))
         ps = ctx.enter_context(tc.psum_pool(name="ps", bufs=1))
 
         def grouped(ap):
@@ -39,12 +40,13 @@ def tile_attend_hvgatedgroups_s_kernel(tc, query, keys_words, keys_scales, th, g
         kw = sb.tile([P, T], U16, name="kw")
         vw = sb.tile([P, T], U16, name="vw")
         ks = sb.tile([P, T], U8, name="ks")
-        vs = sb.tile([P, T], U8, name="vs", tag="codes_go", align_bytes=64)
+        vs = sb.tile([P, T], U8, name="vs")
         th_sb = sb.tile([P, 1], F32, name="th_sb")
         base_sb = sb.tile([P, T], F32, name="base_sb")
         window = sb.tile([P, T], F32, name="window")
         raw = {n: sb.tile([P, PACK, Q], F32, name="raw_" + n, tag="raw_" + n) for n in ("q", "dq", "go")}
-        woven = {n: sb.tile([P, Q, PACK], BF16, name="woven_" + n, tag="woven_" + n, align_bytes=64) for n in ("q", "dq", "go")}
+        woven = {n: sb.tile([P, Q, PACK], BF16, name="woven_" + n, align_bytes=64) for n in ("q", "dq")}
+        woven["go"] = shared.tile([P, Q, PACK], BF16, name="woven_go", align_bytes=64, offset=1024)
         codes = {}
         scales = {n: sb.tile([P, Q], U8, name="scales_" + n, align_bytes=64) for n in ("q", "dq", "go")}
         kwg = sb.tile([P, I], U16, name="kwg", align_bytes=64)
@@ -101,7 +103,12 @@ def tile_attend_hvgatedgroups_s_kernel(tc, query, keys_words, keys_scales, th, g
         nc.scalar.activation(p[:], a[:], ACT.Exp)
         weave("go")
 
-        half4 = sb.tile([P, G, 4], F32, name="half4")
+        nc.vector.tensor_copy(vwg[:], vw[:].indirect(offsets[:]))
+        nc.vector.tensor_copy(vsg[:], vs[:].indirect(offsets[:]))
+        quantize("go")
+        c = product("go", vwg, vsg, "c")
+
+        half4 = shared.tile([P, G, 4], F32, name="half4", offset=256)
         half2 = sb.tile([P, G, 2], F32, name="half2")
         s = sb.tile([P, G], F32, name="s")
         nc.gpsimd.tensor_tensor(half4[:], grouped(p[:])[:, :, 0:4], grouped(p[:])[:, :, 4:8], ALU.add)
@@ -111,40 +118,40 @@ def tile_attend_hvgatedgroups_s_kernel(tc, query, keys_words, keys_scales, th, g
         nc.scalar.activation(root[:], s[:], ACT.Abs_reciprocal_sqrt, bias=eth[:])
         r = sb.tile([P, G], F32, name="r")
         nc.scalar.activation(r[:], root[:], ACT.Square)
-        w = sb.tile([P, I], F32, name="w")
-        nc.gpsimd.tensor_tensor(grouped(w[:]), grouped(p[:]), spread(r[:]), ALU.mult)
 
-        nc.vector.tensor_copy(vwg[:], vw[:].indirect(offsets[:]))
-        nc.vector.tensor_copy(vsg[:], vs[:].indirect(offsets[:]))
-        quantize("go")
-        c = product("go", vwg, vsg, "c")
 
-        sums = sb.tile([P, 3, G], F32, name="sums")
-        tp = sb.tile([P, I], F32, name="tp", tag="woven_go", align_bytes=64)
-        nc.vector.tensor_tensor(tp[:], ta[:], p[:], ALU.mult)
-        pc = sb.tile([P, I], F32, name="pc")
-        nc.vector.tensor_tensor(pc[:], c[:], p[:], ALU.mult)
-        nc.vector.tensor_reduce(sums[:, 0, :], grouped(tp[:]), AX.X, ALU.add)
+        prods = shared.tile([P, 2, I], F32, name="prods", offset=1280)
+        tp, pc = prods[:, 0, :], prods[:, 1, :]
+        nc.vector.tensor_tensor(tp, ta[:], p[:], ALU.mult)
+        nc.vector.tensor_tensor(pc, c[:], p[:], ALU.mult)
         tpc = sb.tile([P, I], F32, name="tpc")
-        nc.vector.tensor_tensor(tpc[:], c[:], tp[:], ALU.mult)
-        nc.vector.tensor_reduce(sums[:, 1, :], grouped(pc[:]), AX.X, ALU.add)
-        nc.vector.tensor_reduce(sums[:, 2, :], grouped(tpc[:]), AX.X, ALU.add)
-        means = sb.tile([P, 3, G], F32, name="means")
-        nc.vector.tensor_tensor(means[:], sums[:], r[:].unsqueeze(1).to_broadcast([P, 3, G]), ALU.mult)
-        u, m, v = means[:, 0, :], means[:, 1, :], means[:, 2, :]
+        nc.vector.tensor_tensor(tpc[:], c[:], tp, ALU.mult)
+        tpc4 = sb.tile([P, G, 4], F32, name="tpc4")
+        nc.gpsimd.tensor_tensor(tpc4[:], grouped(tpc[:])[:, :, 0:4], grouped(tpc[:])[:, :, 4:8], ALU.add)
+        sums = sb.tile([P, 2, G], F32, name="sums", tag="sums")
+        nc.vector.tensor_reduce(sums[:], prods[:].rearrange("p n (g j) -> p n g j", j=GS), AX.X, ALU.add)
+        means = sb.tile([P, 2, G], F32, name="means")
+        nc.vector.tensor_tensor(means[:], sums[:], r[:].unsqueeze(1).to_broadcast([P, 2, G]), ALU.mult)
+        u, m = means[:, 0, :], means[:, 1, :]
+        w = sb.tile([P, I], F32, name="w", tag="sums")
+        nc.gpsimd.tensor_tensor(grouped(w[:]), grouped(p[:]), spread(r[:]), ALU.mult)
+        tdsh = sb.tile([P, G], F32, name="tdsh")
+        nc.vector.tensor_reduce(tdsh[:], tpc4[:], AX.X, ALU.add)
         x = sb.tile([P, I], F32, name="x")
         nc.vector.tensor_tensor(grouped(x[:]), grouped(ta[:]), spread(u), ALU.subtract)
-        um8 = sb.tile([P, G], F32, name="um8")
-        nc.vector.scalar_tensor_tensor(um8[:], u, 8.0, m, ALU.mult, ALU.mult)
         y = sb.tile([P, I], F32, name="y")
         nc.vector.tensor_tensor(grouped(y[:]), grouped(c[:]), spread(m), ALU.subtract)
+        v8 = sb.tile([P, G], F32, name="v8")
+        nc.vector.scalar_tensor_tensor(v8[:], tdsh[:], 8.0, r[:], ALU.mult, ALU.mult)
+        um8 = sb.tile([P, G], F32, name="um8")
+        nc.vector.scalar_tensor_tensor(um8[:], u, 8.0, m, ALU.mult, ALU.mult)
         k8 = sb.tile([P, G], F32, name="k8")
-        nc.vector.scalar_tensor_tensor(k8[:], v, 8.0, um8[:], ALU.mult, ALU.subtract)
         z = sb.tile([P, I], F32, name="z")
         z2 = sb.tile([P, I], F32, name="z2")
         halves = (slice(0, I // 2), slice(I // 2, I))
-        for h in halves:
-            nc.vector.scalar_tensor_tensor(z[:, h], x[:, h], 8.0, y[:, h], ALU.mult, ALU.mult)
+        nc.vector.scalar_tensor_tensor(z[:, halves[0]], x[:, halves[0]], 8.0, y[:, halves[0]], ALU.mult, ALU.mult)
+        nc.vector.tensor_tensor(k8[:], v8[:], um8[:], ALU.subtract)
+        nc.vector.scalar_tensor_tensor(z[:, halves[1]], x[:, halves[1]], 8.0, y[:, halves[1]], ALU.mult, ALU.mult)
         for n, h in enumerate(halves):
             k_half = k8[:, n * G // 2 : (n + 1) * G // 2].unsqueeze(2).to_broadcast([P, G // 2, GS])
             nc.vector.tensor_tensor(grouped(z2[:, h]), grouped(z[:, h]), k_half, ALU.subtract)

from contextlib import ExitStack

import concourse.mybir as mybir

D, E, T, I, Q, G = 512, 512, 2048, 512, 128, 64
GS = I // G
FLOPS = 3 * 2 * 512 * Q * I

F32 = mybir.dt.float32
BF16 = mybir.dt.bfloat16
I32 = mybir.dt.int32
U32 = mybir.dt.uint32
U16 = mybir.dt.uint16
U8 = mybir.dt.uint8
FP8X4 = mybir.dt.float8_e4m3fn_x4
FP4X4 = mybir.dt.float4_e2m1fn_x4
ALU = mybir.AluOpType
ACT = mybir.ActivationFunctionType
AX = mybir.AxisListType

P = 128
PACK = 4
OUT_CHUNKS = (256, 512, 512, 512, 256)


def tile_attend_hvgatedgroups_s_kernel(tc, query, keys_words, keys_scales, th, gout, vals_words, vals_scales, dquery, base, offs, out):
    nc = tc.nc
    with ExitStack() as ctx:
        sb = ctx.enter_context(tc.tile_pool(name="sb", bufs=1))
        shared = ctx.enter_context(tc.tile_pool(name="shared", bufs=1))
        ps = ctx.enter_context(tc.psum_pool(name="ps", bufs=1))

        def grouped(ap):
            return ap.rearrange("p (g j) -> p g j", j=GS)

        def spread(ap):
            return ap.unsqueeze(2).to_broadcast([P, G, GS])

        offsets = sb.tile([P, I // 16], U16, name="offsets")
        kw = sb.tile([P, T], U16, name="kw")
        vw = sb.tile([P, T], U16, name="vw")
        ks = sb.tile([P, T], U8, name="ks")
        vs = sb.tile([P, T], U8, name="vs")
        th_sb = sb.tile([P, 1], F32, name="th_sb")
        base_sb = sb.tile([P, T], F32, name="base_sb")
        window = sb.tile([P, T], F32, name="window")
        raw = {n: sb.tile([P, PACK, Q], F32, name="raw_" + n, tag="raw_" + n) for n in ("q", "dq", "go")}
        woven = {n: sb.tile([P, Q, PACK], BF16, name="woven_" + n, align_bytes=64) for n in ("q", "dq")}
        woven["go"] = shared.tile([P, Q, PACK], BF16, name="woven_go", align_bytes=64, offset=1024)
        codes = {}
        scales = {n: sb.tile([P, Q], U8, name="scales_" + n, align_bytes=64) for n in ("q", "dq", "go")}
        kwg = sb.tile([P, I], U16, name="kwg", align_bytes=64)
        vwg = sb.tile([P, I], U16, name="vwg", align_bytes=64)
        ksg = sb.tile([P, I], U8, name="ksg", align_bytes=64)
        vsg = sb.tile([P, I], U8, name="vsg", align_bytes=64)

        nc.vector.memset(ks[:].bitcast(I32), 0)
        nc.vector.memset(vs[:].bitcast(I32), 0)
        nc.vector.memset(window[:], 0.0)

        def load_scales(tile, src):
            for row in range(4):
                nc.sync.dma_start(out=tile[row:P:32, :].bitcast(I32), in_=src[0, row:16:4, :].bitcast(I32))

        def load_rows(n, src):
            nc.sync.dma_start(out=raw[n][:], in_=src.rearrange("(p j) w -> p j w", j=PACK))

        nc.sync.dma_start(offsets[:], offs)
        nc.scalar.dma_start(out=th_sb[:], in_=th)
        nc.sync.dma_start(out=kw[:].bitcast(I32), in_=keys_words[0].bitcast(I32))
        load_scales(ks, keys_scales)
        load_rows("q", query)
        load_rows("dq", dquery)
        nc.sync.dma_start(out=vw[:].bitcast(I32), in_=vals_words[0].bitcast(I32))
        load_scales(vs, vals_scales)
        load_rows("go", gout)
        nc.sync.dma_start(out=base_sb[:], in_=base)

        eth = sb.tile([P, 1], F32, name="eth")
        nc.scalar.activation(eth[:], th_sb[:], ACT.Exp)

        def weave(n):
            nc.scalar.copy(out=woven[n][:], in_=raw[n][:].rearrange("p j w -> p w j"))

        def quantize(n):
            codes[n] = sb.tile([P, Q], U32, name="codes_" + n, tag="codes_" + n, align_bytes=64)
            nc.vector.quantize_mx(out=codes[n][:].bitcast(FP8X4), scales=scales[n][:], in_=woven[n][:].rearrange("p w j -> p (w j)"))

        def product(n, words, bytes_, name):
            acc = ps.tile([Q, I], F32, name=name)
            nc.tensor.matmul_mx(out=acc[:], lhsT=codes[n][:].bitcast(FP8X4), lhsT_scale=scales[n][:], rhs=words[:].bitcast(FP4X4), rhs_scale=bytes_[:], start=True, stop=True)
            return acc

        weave("q")
        weave("dq")
        nc.vector.tensor_copy(kwg[:], kw[:].indirect(offsets[:]))
        nc.vector.tensor_copy(ksg[:], ks[:].indirect(offsets[:]))
        quantize("q")
        quantize("dq")
        a = product("q", kwg, ksg, "a")
        ta = product("dq", kwg, ksg, "ta")
        p = sb.tile([P, I], F32, name="p")
        nc.scalar.activation(p[:], a[:], ACT.Exp)
        weave("go")

        nc.vector.tensor_copy(vwg[:], vw[:].indirect(offsets[:]))
        nc.vector.tensor_copy(vsg[:], vs[:].indirect(offsets[:]))
        quantize("go")
        c = product("go", vwg, vsg, "c")

        half4 = shared.tile([P, G, 4], F32, name="half4", offset=256)
        half2 = sb.tile([P, G, 2], F32, name="half2")
        s = sb.tile([P, G], F32, name="s")
        nc.gpsimd.tensor_tensor(half4[:], grouped(p[:])[:, :, 0:4], grouped(p[:])[:, :, 4:8], ALU.add)
        nc.gpsimd.tensor_tensor(half2[:], half4[:, :, 0:2], half4[:, :, 2:4], ALU.add)
        nc.gpsimd.tensor_tensor(s[:], half2[:, :, 0], half2[:, :, 1], ALU.add)
        root = sb.tile([P, G], F32, name="root", tag="raw_go")
        nc.scalar.activation(root[:], s[:], ACT.Abs_reciprocal_sqrt, bias=eth[:])
        r = sb.tile([P, G], F32, name="r")
        nc.scalar.activation(r[:], root[:], ACT.Square)


        prods = shared.tile([P, 2, I], F32, name="prods", offset=1280)
        tp, pc = prods[:, 0, :], prods[:, 1, :]
        nc.vector.tensor_tensor(tp, ta[:], p[:], ALU.mult)
        nc.vector.tensor_tensor(pc, c[:], p[:], ALU.mult)
        tpc = sb.tile([P, I], F32, name="tpc")
        nc.vector.tensor_tensor(tpc[:], c[:], tp, ALU.mult)
        tpc4 = sb.tile([P, G, 4], F32, name="tpc4")
        nc.gpsimd.tensor_tensor(tpc4[:], grouped(tpc[:])[:, :, 0:4], grouped(tpc[:])[:, :, 4:8], ALU.add)
        sums = sb.tile([P, 2, G], F32, name="sums", tag="sums")
        nc.vector.tensor_reduce(sums[:], prods[:].rearrange("p n (g j) -> p n g j", j=GS), AX.X, ALU.add)
        means = sb.tile([P, 2, G], F32, name="means")
        nc.vector.tensor_tensor(means[:], sums[:], r[:].unsqueeze(1).to_broadcast([P, 2, G]), ALU.mult)
        u, m = means[:, 0, :], means[:, 1, :]
        w = sb.tile([P, I], F32, name="w", tag="sums")
        nc.gpsimd.tensor_tensor(grouped(w[:]), grouped(p[:]), spread(r[:]), ALU.mult)
        tdsh = sb.tile([P, G], F32, name="tdsh")
        nc.vector.tensor_reduce(tdsh[:], tpc4[:], AX.X, ALU.add)
        x = sb.tile([P, I], F32, name="x")
        nc.vector.tensor_tensor(grouped(x[:]), grouped(ta[:]), spread(u), ALU.subtract)
        y = sb.tile([P, I], F32, name="y")
        nc.vector.tensor_tensor(grouped(y[:]), grouped(c[:]), spread(m), ALU.subtract)
        v8 = sb.tile([P, G], F32, name="v8")
        nc.vector.scalar_tensor_tensor(v8[:], tdsh[:], 8.0, r[:], ALU.mult, ALU.mult)
        um8 = sb.tile([P, G], F32, name="um8")
        nc.vector.scalar_tensor_tensor(um8[:], u, 8.0, m, ALU.mult, ALU.mult)
        k8 = sb.tile([P, G], F32, name="k8")
        z = sb.tile([P, I], F32, name="z")
        z2 = sb.tile([P, I], F32, name="z2")
        halves = (slice(0, I // 2), slice(I // 2, I))
        nc.vector.scalar_tensor_tensor(z[:, halves[0]], x[:, halves[0]], 8.0, y[:, halves[0]], ALU.mult, ALU.mult)
        nc.vector.tensor_tensor(k8[:], v8[:], um8[:], ALU.subtract)
        nc.vector.scalar_tensor_tensor(z[:, halves[1]], x[:, halves[1]], 8.0, y[:, halves[1]], ALU.mult, ALU.mult)
        for n, h in enumerate(halves):
            k_half = k8[:, n * G // 2 : (n + 1) * G // 2].unsqueeze(2).to_broadcast([P, G // 2, GS])
            nc.vector.tensor_tensor(grouped(z2[:, h]), grouped(z[:, h]), k_half, ALU.subtract)
        nc.vector.tensor_tensor(window[:].indirect(offsets[:]), z2[:], w[:], ALU.mult)

        res = sb.tile([P, T], F32, name="res")
        col = 0
        for n, width in enumerate(OUT_CHUNKS):
            cols = slice(col, col + width)
            nc.vector.tensor_tensor(res[:, cols], window[:, cols], base_sb[:, cols], ALU.add)
            queue = nc.sync if n % 2 == 0 else nc.scalar
            queue.dma_start(out=out[:, cols], in_=res[:, cols])
            col = col + width
